import numpy as np
import ml_dtypes


def mxq(x, axis, fmt="e4m3"):
    dtype, down = {"e4m3": (ml_dtypes.float8_e4m3fn, 7), "e5m2": (ml_dtypes.float8_e5m2, 14)}[fmt]
    v = np.moveaxis(np.asarray(x, np.float32).astype(ml_dtypes.bfloat16).astype(np.float64), axis, -1)
    blocks = v.reshape(v.shape[:-1] + (-1, 32))
    amax = np.abs(blocks).max(-1, keepdims=True)
    byte = np.maximum(np.where(amax > 0, np.frexp(amax)[1] - 1 + 127, 0) - down, 1)
    scale = np.exp2(byte - 127.0)
    codes = (blocks / scale).astype(np.float32).astype(dtype).astype(np.float64)
    return np.moveaxis((codes * scale).reshape(v.shape), -1, axis)


WIDE = False


def mx_kscale(k):
    if not WIDE:
        return np.ones(k)
    levels = np.array([10, -10, 5, -5, 0])
    if k % 512:
        return np.exp2(np.random.permutation(np.resize(levels, k // 32))).repeat(32)
    a = np.empty((k // 512, 16))
    for p in range(k // 512):
        a[p, :8] = np.random.permutation(np.resize(levels, 8))
        for g in range(8):
            far = levels[np.abs(levels - a[p, g]) >= 10]
            a[p, g + 8] = far[np.random.randint(len(far))]
    return np.exp2(a.ravel()).repeat(32)


def f64(x):
    return np.asarray(x).astype(np.float64)


E2M1 = np.array([0.0, 0.5, 1.0, 1.5, 2.0, 3.0, 4.0, 6.0, -0.0, -0.5, -1.0, -1.5, -2.0, -3.0, -4.0, -6.0])


def pack_weight(w, fmt):
    k, n = w.shape
    w = f64(np.asarray(w, np.float32).astype(ml_dtypes.bfloat16)).reshape(k // 32, 32, n)
    amax = np.abs(w).max(1)
    if fmt == "e4m3":
        byte = np.frexp(amax)[1] - 1 + 127 - 7
    else:
        mant, ex = np.frexp(amax / 6.0)
        byte = np.where(mant > 0.5, ex, ex - 1) + 127
    byte = np.clip(np.where(amax > 0, byte, 1), 1, 254)
    scaled = (w * np.exp2(127.0 - byte)[:, None, :]).reshape(k, n).astype(np.float32)
    by_word = np.ascontiguousarray(scaled.reshape(k // 512, 128, 4, n).transpose(0, 1, 3, 2))
    if fmt == "e4m3":
        words = by_word.astype(ml_dtypes.float8_e4m3fn).view(np.uint8)
    else:
        c = by_word.astype(ml_dtypes.float4_e2m1fn).view(np.uint8) & 0xF
        words = (c[..., 0::2] | (c[..., 1::2] << 4)).reshape(k // 512, 128, 2 * n)
    return np.ascontiguousarray(words), np.ascontiguousarray(byte.astype(np.uint8).reshape(k // 512, 16, n))


def unpack_weight(words, scales, fmt):
    g, _, n = scales.shape
    words = np.ascontiguousarray(words).reshape(g, 128, n, -1)
    if fmt == "e4m3":
        vals = words.view(ml_dtypes.float8_e4m3fn).astype(np.float64)
    else:
        nib = np.empty((g, 128, n, 4), np.uint8)
        nib[..., 0::2] = words & 0xF
        nib[..., 1::2] = words >> 4
        vals = E2M1[nib]
    vals = vals * np.repeat(np.exp2(scales.astype(np.float64) - 127.0), 8, axis=1)[..., None]
    return vals.transpose(0, 1, 3, 2).reshape(g * 512, n)


def bf(x):
    return np.asarray(x, np.float32).astype(ml_dtypes.bfloat16)


def planes(Y):
    r, m = Y.shape
    b = f64(bf(Y)).reshape(r // 32, 32, m)
    amax = np.abs(b).max(1)
    byte = np.clip(np.where(amax > 0, np.frexp(amax)[1] - 1 + 127 - 7, 1), 1, 254)
    codes = (b * np.exp2(127.0 - byte)[:, None, :]).reshape(r, m).astype(np.float32).astype(ml_dtypes.float8_e4m3fn).view(np.uint8)
    words = codes.reshape(r // 512, 128, 4, m).transpose(0, 1, 3, 2)
    return np.ascontiguousarray(words), np.ascontiguousarray(byte.astype(np.uint8).reshape(r // 512, 16, m))


K, L, T, R, N = 1024, 512, 512, 512, 512


def setup_inputs():
    n = np.random.standard_normal
    fk = mx_kscale(K)
    fl = mx_kscale(L)
    fr = mx_kscale(R)
    xtp = pack_weight(n((K, T)) * np.random.uniform(0.3, 1.9, (1, T)) / fk[:, None], "e4m3")
    wap = pack_weight(n((K, R)) * 1 / np.sqrt(K) * fk[:, None], "e4m3")
    xqp = pack_weight(n((L, T)) * 0.5 / fl[:, None], "e2m1")
    wcp = pack_weight(n((L, R)) * 1 / np.sqrt(L) * fl[:, None], "e2m1")
    wbp = pack_weight(n((R, N)) * 1 / np.sqrt(R) / fr[:, None], "e4m3")
    wyp = pack_weight(n((K, N)) * 1 / np.sqrt(K) * fk[:, None], "e2m1")
    return {
        "xt_words": xtp[0],
        "xt_scales": xtp[1],
        "wa_words": wap[0],
        "wa_scales": wap[1],
        "xq_words": xqp[0],
        "xq_scales": xqp[1],
        "wc_words": wcp[0],
        "wc_scales": wcp[1],
        "fr": (np.random.uniform(0.5, 2.0, (R, 1)) * fr[:, None]).astype(np.float32),
        "wb_words": wbp[0],
        "wb_scales": wbp[1],
        "wy_words": wyp[0],
        "wy_scales": wyp[1],
    }


def reference(xt_words, xt_scales, wa_words, wa_scales, xq_words, xq_scales, wc_words, wc_scales, fr, wb_words, wb_scales, wy_words, wy_scales):
    xtu = unpack_weight(xt_words, xt_scales, "e4m3")
    wau = unpack_weight(wa_words, wa_scales, "e4m3")
    xqu = unpack_weight(xq_words, xq_scales, "e2m1")
    wcu = unpack_weight(wc_words, wc_scales, "e2m1")
    wbu = unpack_weight(wb_words, wb_scales, "e4m3")
    wyu = unpack_weight(wy_words, wy_scales, "e2m1")
    z = xtu.T @ wau + xqu.T @ wcu
    e = np.mean(np.square(z), axis=1, keepdims=True)
    h1 = z * e / (e + 1.0)
    ht = h1.T
    hid = ht * f64(fr)
    hidq = mxq(hid, 0, "e4m3")
    y = wbu.T @ hidq + wyu.T @ xtu
    words, scales = planes(y)
    return y, words, scales

@@ -1,0 +1,311 @@
+from contextlib import ExitStack
+
+import concourse.mybir as mybir
+from concourse.masks import make_identity
+
+K, L, T, R, N = 1024, 512, 512, 512, 512
+FLOPS = 2 * T * (K * R + L * R + R * N + K * N)
+
+F32 = mybir.dt.float32
+BF16 = mybir.dt.bfloat16
+I32 = mybir.dt.int32
+U32 = mybir.dt.uint32
+U8 = mybir.dt.uint8
+FP8X4 = mybir.dt.float8_e4m3fn_x4
+FP4X4 = mybir.dt.float4_e2m1fn_x4
+ALU = mybir.AluOpType
+ACT = mybir.ActivationFunctionType
+
+P = 128
+PACK = 4
+W = 512
+TILES = T // P
+QUADS = 4
+
+XQ, WC, XT, WA, WY, WB = 0, 1, 2, 4, 6, 8
+PLANES = 9
+
+
+def tile_mix_hidden_by_row_energy_pl_kernel(
+    tc, xt_words, xt_scales, wa_words, wa_scales, xq_words, xq_scales, wc_words, wc_scales,
+    fr, wb_words, wb_scales, wy_words, wy_scales, out_0, out_1, out_2,
+):
+    nc = tc.nc
+
+    with ExitStack() as ctx:
+        sb = ctx.enter_context(tc.tile_pool(name="sb", bufs=1))
+        ps = ctx.enter_context(tc.psum_pool(name="ps", bufs=1))
+        ctx.enter_context(tc.manual_schedule())
+
+        def sbuf(name, shape, dtype):
+            return sb.tile(shape, dtype, name=name, align_bytes=64)
+
+        def bank(name, tag, shape):
+            return ps.tile(shape, F32, name=name, tag=tag)
+
+        fr_col = sbuf("fr_col", [P, PACK], F32)
+        nc.gpsimd.dma_start(out=fr_col[:], in_=fr.rearrange("(p j) o -> p (j o)", j=PACK))
+        ident = sbuf("ident", [P, P], F32)
+        make_identity(nc, ident[:])
+
+        planes = sbuf("planes", [P, PLANES * W], U8)
+        nc.vector.memset(planes[:].bitcast(I32), 0)
+
+        staged = sbuf("staged", [16, PLANES * W], U8)
+        staged_words = staged[:].bitcast(I32).rearrange("q (z c) -> q z c", z=PLANES)
+        for first, scales in ((XQ, xq_scales), (WC, wc_scales), (XT, xt_scales), (WA, wa_scales),
+                              (WY, wy_scales), (WB, wb_scales)):
+            passes = scales.shape[0]
+            nc.scalar.dma_start(
+                out=staged_words[:, first : first + passes, :],
+                in_=scales.bitcast(I32).rearrange("z q c -> q z c"),
+            )
+
+        def fp8_words(words):
+            return words.rearrange("z p c r -> p z (c r)").bitcast(I32)
+
+        def fp4_words(words):
+            return words.bitcast(I32).rearrange("z p c -> p z c")
+
+        wy_raw = sbuf("wy_raw", [P, 2, 2 * W], U8)
+        nc.sync.dma_start(out=wy_raw[:].bitcast(I32), in_=fp4_words(wy_words))
+        xt = sbuf("xt", [P, 2, W], U32)
+        nc.sync.dma_start(out=xt[:].bitcast(I32), in_=fp8_words(xt_words))
+        xq = sbuf("xq", [P, 2 * W], U8)
+        nc.sync.dma_start(out=xq[:].bitcast(I32), in_=fp4_words(xq_words)[:, 0, :])
+        wc = sbuf("wc", [P, 2 * W], U8)
+        nc.sync.dma_start(out=wc[:].bitcast(I32), in_=fp4_words(wc_words)[:, 0, :])
+        wa = []
+        for z in range(2):
+            wa_z = sbuf("wa%d" % z, [P, W], U32)
+            nc.sync.dma_start(out=wa_z[:].bitcast(I32), in_=fp8_words(wa_words)[:, z, :])
+            wa.append(wa_z)
+        wb_raw = sbuf("wb_raw", [P, W], U32)
+        nc.sync.dma_start(out=wb_raw[:].bitcast(I32), in_=fp8_words(wb_words)[:, 0, :])
+
+        for q in range(QUADS):
+            nc.scalar.dma_start(
+                out=planes[32 * q : 32 * q + 4, :].bitcast(I32),
+                in_=staged[4 * q : 4 * q + 4, :].bitcast(I32),
+            )
+
+        def plane(index, cols):
+            return planes[:, index * W + cols.start : index * W + cols.stop]
+
+        fr_ps = bank("fr_ps", "y3", [P, PACK, P])
+        for j in range(PACK):
+            nc.tensor.transpose(fr_ps[:, j, :], fr_col[:, j : j + 1].to_broadcast([P, P]), ident[:])
+        fr_row = sbuf("fr_row", [P, 2, P, 2], F32)
+        nc.scalar.activation(
+            out=fr_row[:], in_=fr_ps[:].rearrange("m (u e) p -> m u p e", e=2), func=ACT.Copy)
+
+        wy = sbuf("wy", [P, 2, 2 * W], U8)
+        nc.vector.tensor_copy(
+            out=wy[:].rearrange("p z (i m b) -> p z i m b", i=PACK, b=2),
+            in_=wy_raw[:].rearrange("p z (m i b) -> p z i m b", i=PACK, b=2),
+        )
+        dealt = sbuf("dealt", [P, 3 * W], U8)
+        nc.vector.tensor_copy(
+            out=dealt[:, 0 : 2 * W].rearrange("p (z i m) -> p z i m", z=2, i=PACK),
+            in_=planes[:, WY * W : WB * W].rearrange("p (z m i) -> p z i m", z=2, i=PACK),
+        )
+        nc.vector.tensor_copy(
+            out=dealt[:, 2 * W : 3 * W].rearrange("p (i m) -> p i m", i=PACK),
+            in_=planes[:, WB * W : PLANES * W].rearrange("p (m i) -> p i m", i=PACK),
+        )
+        wb = sbuf("wb", [P, W], U32)
+        nc.vector.tensor_copy(
+            out=wb[:].bitcast(I32).rearrange("p (i m) -> p i m", i=PACK),
+            in_=wb_raw[:].bitcast(I32).rearrange("p (m i) -> p i m", i=PACK),
+        )
+
+        all_cols = slice(0, W)
+        tok = [slice(j * P, (j + 1) * P) for j in range(TILES)]
+        z_ps = [bank("z%d" % j, "z%d" % j, [P, W]) for j in range(TILES)]
+        y_ps = {}
+        turned = {}
+        squares = sbuf("squares", [P, W], BF16)
+        sums = sbuf("sums", [P, TILES], F32)
+        denom = sbuf("denom", [P, TILES], F32)
+        recip = sbuf("recip", [P, TILES], F32)
+        gain = sbuf("gain", [P, TILES], F32)
+        hid_rows = [sbuf("hid_rows%d" % j, [P, 2, 2 * P], BF16) for j in range(TILES)]
+        hid_cols = [sbuf("hid_cols%d" % j, [P, W], BF16) for j in range(TILES)]
+        hid_codes = sbuf("hid_codes", [P, W], U32)
+        hid_plane = sbuf("hid_plane", [P, W], U8)
+        y_out = [sbuf("y_out%d" % j, [P, PACK, P], F32) for j in range(TILES)]
+        y_cols = [sbuf("y_cols%d" % j, [P, W], BF16) for j in range(TILES)]
+        y_codes = sbuf("y_codes", [P, W], U32)
+        y_plane = sbuf("y_plane", [P, W], U8)
+        out0_view = out_0.rearrange("(p i) t -> p i t", i=PACK)
+        out1_view = out_1[0].rearrange("p c r -> p (c r)").bitcast(I32)
+
+        def z_fp4(j):
+            nc.tensor.matmul_mx(
+                out=z_ps[j][:],
+                lhsT=xq[:, 2 * j * P : 2 * (j + 1) * P].bitcast(FP4X4), lhsT_scale=plane(XQ, tok[j]),
+                rhs=wc[:].bitcast(FP4X4), rhs_scale=plane(WC, all_cols),
+                start=True, stop=False,
+            )
+
+        def z_fp8(j):
+            for z in range(2):
+                nc.tensor.matmul_mx(
+                    out=z_ps[j][:],
+                    lhsT=xt[:, z, tok[j]].bitcast(FP8X4), lhsT_scale=plane(XT + z, tok[j]),
+                    rhs=wa[z][:].bitcast(FP8X4), rhs_scale=plane(WA + z, all_cols),
+                    start=False, stop=(z == 1),
+                )
+
+        def energy(j):
+            nc.scalar.activation(out=squares[:], in_=z_ps[j][:], func=ACT.Square, accum_out=sums[:, j : j + 1])
+
+        def gain_sum(j):
+            col = slice(j, j + 1)
+            nc.vector.tensor_scalar(out=denom[:, col], in0=sums[:, col], scalar1=float(R), scalar2=None, op0=ALU.add)
+
+        def gain_recip(j):
+            col = slice(j, j + 1)
+            nc.vector.reciprocal(out=recip[:, col], in_=denom[:, col])
+
+        def gain_mult(j):
+            col = slice(j, j + 1)
+            nc.vector.tensor_tensor(out=gain[:, col], in0=sums[:, col], in1=recip[:, col], op=ALU.mult)
+
+        def weigh(j, u):
+            nc.vector.scalar_tensor_tensor(
+                out=hid_rows[j][:, u, :].rearrange("t (p e) -> t p e", e=2),
+                in0=z_ps[j][:].rearrange("t (p i) -> t p i", i=PACK)[:, :, 2 * u : 2 * u + 2],
+                scalar=gain[:, j : j + 1],
+                in1=fr_row[:, u, :, :],
+                op0=ALU.mult, op1=ALU.mult,
+            )
+
+        def turn(j):
+            turned[j] = bank("turned%d" % j, "z%d" % j, [P, 2, P])
+            for u in range(2):
+                nc.tensor.transpose(turned[j][:, u, :], hid_rows[j][:, u, :].bitcast(F32), ident[:])
+
+        def gather_words(j):
+            nc.scalar.copy(
+                out=hid_cols[j][:].bitcast(F32).rearrange("p (t u) -> p t u", u=2),
+                in_=turned[j][:].rearrange("p u t -> p t u"),
+            )
+
+        def quantise_hid(j):
+            nc.vector.quantize_mx(
+                out=hid_codes[:, tok[j]].bitcast(FP8X4), scales=hid_plane[:, tok[j]], in_=hid_cols[j][:])
+
+        def skip(j):
+            y_ps[j] = bank("y%d" % j, "y%d" % j, [P, PACK, P])
+            for z in range(2):
+                for i in range(PACK):
+                    nc.tensor.matmul_mx(
+                        out=y_ps[j][:, i, :],
+                        lhsT=wy[:, z, 2 * i * P : 2 * (i + 1) * P].bitcast(FP4X4),
+                        lhsT_scale=dealt[:, z * W + i * P : z * W + (i + 1) * P],
+                        rhs=xt[:, z, tok[j]].bitcast(FP8X4), rhs_scale=plane(XT + z, tok[j]),
+                        start=(z == 0 and i == 0), stop=False,
+                    )
+
+        def second(j):
+            for i in range(PACK):
+                nc.tensor.matmul_mx(
+                    out=y_ps[j][:, i, :],
+                    lhsT=wb[:, i * P : (i + 1) * P].bitcast(FP8X4),
+                    lhsT_scale=dealt[:, 2 * W + i * P : 2 * W + (i + 1) * P],
+                    rhs=hid_codes[:, tok[j]].bitcast(FP8X4), rhs_scale=hid_plane[:, tok[j]],
+                    start=False, stop=(i == PACK - 1),
+                )
+
+        def drain(j):
+            nc.scalar.copy(out=y_out[j][:], in_=y_ps[j][:])
+            nc.sync.dma_start(out=out0_view[:, :, tok[j]], in_=y_out[j][:])
+
+        def interleave(j):
+            nc.vector.tensor_copy(
+                out=y_cols[j][:].rearrange("p (t i) -> p t i", i=PACK),
+                in_=y_out[j][:].rearrange("p i t -> p t i"),
+            )
+
+        def interleave_from_psum(j):
+            nc.vector.tensor_copy(
+                out=y_cols[j][:].rearrange("p (t i) -> p t i", i=PACK),
+                in_=y_ps[j][:].rearrange("p i t -> p t i"),
+            )
+
+        def quantise_y(j):
+            nc.vector.quantize_mx(
+                out=y_codes[:, tok[j]].bitcast(FP8X4), scales=y_plane[:, tok[j]], in_=y_cols[j][:])
+            nc.sync.dma_start(out=out1_view[:, tok[j]], in_=y_codes[:, tok[j]].bitcast(I32))
+
+        z_fp4(0)
+        z_fp8(0)
+        energy(0)
+        z_fp4(1)
+        z_fp8(1)
+        energy(1)
+        z_fp4(2)
+        z_fp8(2)
+        energy(2)
+        z_fp4(3)
+        z_fp8(3)
+        energy(3)
+        gain_sum(0)
+        gain_recip(0)
+        gain_mult(0)
+        gain_sum(1)
+        weigh(0, 0)
+        gain_recip(1)
+        weigh(0, 1)
+        gain_mult(1)
+        gain_sum(2)
+        weigh(1, 0)
+        gain_recip(2)
+        weigh(1, 1)
+        gain_mult(2)
+        gain_sum(3)
+        weigh(2, 0)
+        gain_recip(3)
+        weigh(2, 1)
+        gain_mult(3)
+        skip(0)
+        turn(0)
+        gather_words(0)
+        quantise_hid(0)
+        weigh(3, 0)
+        weigh(3, 1)
+        skip(1)
+        turn(1)
+        turn(2)
+        gather_words(1)
+        gather_words(2)
+        second(0)
+        drain(0)
+        quantise_hid(1)
+        quantise_hid(2)
+        skip(2)
+        turn(3)
+        gather_words(3)
+        second(1)
+        drain(1)
+        interleave(0)
+        quantise_hid(3)
+        quantise_y(0)
+        skip(3)
+        second(2)
+        second(3)
+        interleave(1)
+        drain(2)
+        quantise_y(1)
+        interleave_from_psum(3)
+        drain(3)
+        interleave(2)
+        quantise_y(3)
+        quantise_y(2)
+        for q in range(QUADS):
+            queue = nc.scalar if q % 2 else nc.sync
+            queue.dma_start(
+                out=out_2[0, 4 * q : 4 * q + 4, :].bitcast(I32),
+                in_=y_plane[32 * q : 32 * q + 4, :].bitcast(I32),
+            )

@@ -24,6 +24,7 @@ QUADS = 4
 
 XQ, WC, XT, WA, WY, WB = 0, 1, 2, 4, 6, 8
 PLANES = 9
+WARM_PASSES = 22
 
 
 def tile_mix_hidden_by_row_energy_pl_kernel(
@@ -48,15 +49,28 @@ def tile_mix_hidden_by_row_energy_pl_kernel(
         ident = sbuf("ident", [P, P], F32)
         make_identity(nc, ident[:])
 
+        zeros = sbuf("zeros", [P, W], BF16)
+        nc.vector.memset(zeros[:], 0.0)
         planes = sbuf("planes", [P, PLANES * W], U8)
         nc.vector.memset(planes[:].bitcast(I32), 0)
+        warm_codes = sbuf("warm_codes", [P, P], U32)
+        warm_plane = sbuf("warm_plane", [P, P], U8)
+        nc.vector.quantize_mx(out=warm_codes[:].bitcast(FP8X4), scales=warm_plane[:], in_=zeros[:])
+        warm_ps = bank("warm_ps", "y2", [P, P])
+        for rep in range(WARM_PASSES):
+            nc.tensor.matmul_mx(
+                out=warm_ps[:], lhsT=warm_codes[:].bitcast(FP8X4), lhsT_scale=warm_plane[:],
+                rhs=warm_codes[:].bitcast(FP8X4), rhs_scale=warm_plane[:], start=True, stop=True,
+            )
 
         staged = sbuf("staged", [16, PLANES * W], U8)
         staged_words = staged[:].bitcast(I32).rearrange("q (z c) -> q z c", z=PLANES)
-        for first, scales in ((XQ, xq_scales), (WC, wc_scales), (XT, xt_scales), (WA, wa_scales),
-                              (WY, wy_scales), (WB, wb_scales)):
+        for first, scales, queue in (
+            (XQ, xq_scales, nc.sync), (WC, wc_scales, nc.scalar), (XT, xt_scales, nc.sync),
+            (WA, wa_scales, nc.scalar), (WY, wy_scales, nc.sync), (WB, wb_scales, nc.scalar),
+        ):
             passes = scales.shape[0]
-            nc.scalar.dma_start(
+            queue.dma_start(
                 out=staged_words[:, first : first + passes, :],
                 in_=scales.bitcast(I32).rearrange("z q c -> q z c"),
             )
@@ -67,27 +81,24 @@ def tile_mix_hidden_by_row_energy_pl_kernel(
         def fp4_words(words):
             return words.bitcast(I32).rearrange("z p c -> p z c")
 
-        wy_raw = sbuf("wy_raw", [P, 2, 2 * W], U8)
-        nc.sync.dma_start(out=wy_raw[:].bitcast(I32), in_=fp4_words(wy_words))
         xt = sbuf("xt", [P, 2, W], U32)
-        nc.sync.dma_start(out=xt[:].bitcast(I32), in_=fp8_words(xt_words))
+        nc.scalar.dma_start(out=xt[:].bitcast(I32), in_=fp8_words(xt_words))
+        wa = sbuf("wa", [P, 2, W], U32)
+        nc.scalar.dma_start(out=wa[:].bitcast(I32), in_=fp8_words(wa_words))
         xq = sbuf("xq", [P, 2 * W], U8)
-        nc.sync.dma_start(out=xq[:].bitcast(I32), in_=fp4_words(xq_words)[:, 0, :])
+        nc.scalar.dma_start(out=xq[:].bitcast(I32), in_=fp4_words(xq_words)[:, 0, :])
         wc = sbuf("wc", [P, 2 * W], U8)
-        nc.sync.dma_start(out=wc[:].bitcast(I32), in_=fp4_words(wc_words)[:, 0, :])
-        wa = []
-        for z in range(2):
-            wa_z = sbuf("wa%d" % z, [P, W], U32)
-            nc.sync.dma_start(out=wa_z[:].bitcast(I32), in_=fp8_words(wa_words)[:, z, :])
-            wa.append(wa_z)
-        wb_raw = sbuf("wb_raw", [P, W], U32)
-        nc.sync.dma_start(out=wb_raw[:].bitcast(I32), in_=fp8_words(wb_words)[:, 0, :])
+        nc.scalar.dma_start(out=wc[:].bitcast(I32), in_=fp4_words(wc_words)[:, 0, :])
 
         for q in range(QUADS):
-            nc.scalar.dma_start(
+            nc.sync.dma_start(
                 out=planes[32 * q : 32 * q + 4, :].bitcast(I32),
                 in_=staged[4 * q : 4 * q + 4, :].bitcast(I32),
             )
+        wy_raw = sbuf("wy_raw", [P, 2, 2 * W], U8)
+        nc.sync.dma_start(out=wy_raw[:].bitcast(I32), in_=fp4_words(wy_words))
+        wb_raw = sbuf("wb_raw", [P, W], U32)
+        nc.sync.dma_start(out=wb_raw[:].bitcast(I32), in_=fp8_words(wb_words)[:, 0, :])
 
         def plane(index, cols):
             return planes[:, index * W + cols.start : index * W + cols.stop]
@@ -100,24 +111,31 @@ def tile_mix_hidden_by_row_energy_pl_kernel(
             out=fr_row[:], in_=fr_ps[:].rearrange("m (u e) p -> m u p e", e=2), func=ACT.Copy)
 
         wy = sbuf("wy", [P, 2, 2 * W], U8)
-        nc.vector.tensor_copy(
-            out=wy[:].rearrange("p z (i m b) -> p z i m b", i=PACK, b=2),
-            in_=wy_raw[:].rearrange("p z (m i b) -> p z i m b", i=PACK, b=2),
-        )
         dealt = sbuf("dealt", [P, 3 * W], U8)
-        nc.vector.tensor_copy(
-            out=dealt[:, 0 : 2 * W].rearrange("p (z i m) -> p z i m", z=2, i=PACK),
-            in_=planes[:, WY * W : WB * W].rearrange("p (z m i) -> p z i m", z=2, i=PACK),
-        )
-        nc.vector.tensor_copy(
-            out=dealt[:, 2 * W : 3 * W].rearrange("p (i m) -> p i m", i=PACK),
-            in_=planes[:, WB * W : PLANES * W].rearrange("p (m i) -> p i m", i=PACK),
-        )
         wb = sbuf("wb", [P, W], U32)
-        nc.vector.tensor_copy(
-            out=wb[:].bitcast(I32).rearrange("p (i m) -> p i m", i=PACK),
-            in_=wb_raw[:].bitcast(I32).rearrange("p (m i) -> p i m", i=PACK),
-        )
+
+        def deal_wy(part):
+            z, half = divmod(part, 2)
+            nc.vector.tensor_copy(
+                out=wy[:, z, half * W : (half + 1) * W].rearrange("p (i m b) -> p i m b", i=2, b=2),
+                in_=wy_raw[:, z, :].rearrange("p (m i b) -> p i m b", i=PACK, b=2)[:, 2 * half : 2 * half + 2, :, :],
+            )
+
+        def deal_planes():
+            nc.vector.tensor_copy(
+                out=dealt[:, 0 : 2 * W].rearrange("p (z i m) -> p z i m", z=2, i=PACK),
+                in_=planes[:, WY * W : WB * W].rearrange("p (z m i) -> p z i m", z=2, i=PACK),
+            )
+            nc.vector.tensor_copy(
+                out=dealt[:, 2 * W : 3 * W].rearrange("p (i m) -> p i m", i=PACK),
+                in_=planes[:, WB * W : PLANES * W].rearrange("p (m i) -> p i m", i=PACK),
+            )
+
+        def deal_wb():
+            nc.vector.tensor_copy(
+                out=wb[:].bitcast(I32).rearrange("p (i m) -> p i m", i=PACK),
+                in_=wb_raw[:].bitcast(I32).rearrange("p (m i) -> p i m", i=PACK),
+            )
 
         all_cols = slice(0, W)
         tok = [slice(j * P, (j + 1) * P) for j in range(TILES)]
@@ -145,7 +163,7 @@ def tile_mix_hidden_by_row_energy_pl_kernel(
                 out=z_ps[j][:],
                 lhsT=xq[:, 2 * j * P : 2 * (j + 1) * P].bitcast(FP4X4), lhsT_scale=plane(XQ, tok[j]),
                 rhs=wc[:].bitcast(FP4X4), rhs_scale=plane(WC, all_cols),
-                start=True, stop=False,
+                start=False, stop=True,
             )
 
         def z_fp8(j):
@@ -153,8 +171,8 @@ def tile_mix_hidden_by_row_energy_pl_kernel(
                 nc.tensor.matmul_mx(
                     out=z_ps[j][:],
                     lhsT=xt[:, z, tok[j]].bitcast(FP8X4), lhsT_scale=plane(XT + z, tok[j]),
-                    rhs=wa[z][:].bitcast(FP8X4), rhs_scale=plane(WA + z, all_cols),
-                    start=False, stop=(z == 1),
+                    rhs=wa[:, z, :].bitcast(FP8X4), rhs_scale=plane(WA + z, all_cols),
+                    start=(z == 0), stop=False,
                 )
 
         def energy(j):
@@ -237,23 +255,30 @@ def tile_mix_hidden_by_row_energy_pl_kernel(
         def quantise_y(j):
             nc.vector.quantize_mx(
                 out=y_codes[:, tok[j]].bitcast(FP8X4), scales=y_plane[:, tok[j]], in_=y_cols[j][:])
-            nc.sync.dma_start(out=out1_view[:, tok[j]], in_=y_codes[:, tok[j]].bitcast(I32))
+            if j % 2:
+                pair = slice((j - 1) * P, (j + 1) * P)
+                nc.sync.dma_start(out=out1_view[:, pair], in_=y_codes[:, pair].bitcast(I32))
 
-        z_fp4(0)
+        deal_planes()
         z_fp8(0)
+        z_fp8(1)
+        z_fp4(0)
         energy(0)
         z_fp4(1)
-        z_fp8(1)
         energy(1)
-        z_fp4(2)
         z_fp8(2)
+        z_fp4(2)
         energy(2)
-        z_fp4(3)
         z_fp8(3)
+        z_fp4(3)
         energy(3)
+        deal_wy(0)
         gain_sum(0)
+        deal_wy(1)
         gain_recip(0)
+        deal_wy(2)
         gain_mult(0)
+        deal_wy(3)
         gain_sum(1)
         weigh(0, 0)
         gain_recip(1)
@@ -264,6 +289,7 @@ def tile_mix_hidden_by_row_energy_pl_kernel(
         gain_recip(2)
         weigh(1, 1)
         gain_mult(2)
+        deal_wb()
         gain_sum(3)
         weigh(2, 0)
         gain_recip(3)
@@ -292,17 +318,17 @@ def tile_mix_hidden_by_row_energy_pl_kernel(
         interleave(0)
         quantise_hid(3)
         quantise_y(0)
-        skip(3)
         second(2)
+        skip(3)
         second(3)
         interleave(1)
         drain(2)
         quantise_y(1)
-        interleave_from_psum(3)
         drain(3)
         interleave(2)
-        quantise_y(3)
         quantise_y(2)
+        interleave(3)
+        quantise_y(3)
         for q in range(QUADS):
             queue = nc.scalar if q % 2 else nc.sync
             queue.dma_start(

@@ -24,7 +24,7 @@ QUADS = 4
 
 XQ, WC, XT, WA, WY, WB = 0, 1, 2, 4, 6, 8
 PLANES = 9
-WARM_PASSES = 22
+WARM_PASSES = 30
 
 
 def tile_mix_hidden_by_row_energy_pl_kernel(
@@ -63,8 +63,8 @@ def tile_mix_hidden_by_row_energy_pl_kernel(
                 rhs=warm_codes[:].bitcast(FP8X4), rhs_scale=warm_plane[:], start=True, stop=True,
             )
 
-        staged = sbuf("staged", [16, PLANES * W], U8)
-        staged_words = staged[:].bitcast(I32).rearrange("q (z c) -> q z c", z=PLANES)
+        staged = sbuf("staged", [P, PLANES * W], U8)
+        staged_words = staged[4:P:8, :].bitcast(I32).rearrange("q (z c) -> q z c", z=PLANES)
         for first, scales, queue in (
             (XQ, xq_scales, nc.sync), (WC, wc_scales, nc.scalar), (XT, xt_scales, nc.sync),
             (WA, wa_scales, nc.scalar), (WY, wy_scales, nc.sync), (WB, wb_scales, nc.scalar),
@@ -81,6 +81,8 @@ def tile_mix_hidden_by_row_energy_pl_kernel(
         def fp4_words(words):
             return words.bitcast(I32).rearrange("z p c -> p z c")
 
+        wy_raw = sbuf("wy_raw", [P, 2, 2 * W], U8)
+        nc.scalar.dma_start(out=wy_raw[:].bitcast(I32), in_=fp4_words(wy_words))
         xt = sbuf("xt", [P, 2, W], U32)
         nc.scalar.dma_start(out=xt[:].bitcast(I32), in_=fp8_words(xt_words))
         wa = sbuf("wa", [P, 2, W], U32)
@@ -90,13 +92,11 @@ def tile_mix_hidden_by_row_energy_pl_kernel(
         wc = sbuf("wc", [P, 2 * W], U8)
         nc.scalar.dma_start(out=wc[:].bitcast(I32), in_=fp4_words(wc_words)[:, 0, :])
 
-        for q in range(QUADS):
+        for r in range(4):
             nc.sync.dma_start(
-                out=planes[32 * q : 32 * q + 4, :].bitcast(I32),
-                in_=staged[4 * q : 4 * q + 4, :].bitcast(I32),
+                out=planes[r:P:32, :].bitcast(I32),
+                in_=staged[8 * r + 4 : P : 32, :].bitcast(I32),
             )
-        wy_raw = sbuf("wy_raw", [P, 2, 2 * W], U8)
-        nc.sync.dma_start(out=wy_raw[:].bitcast(I32), in_=fp4_words(wy_words))
         wb_raw = sbuf("wb_raw", [P, W], U32)
         nc.sync.dma_start(out=wb_raw[:].bitcast(I32), in_=fp8_words(wb_words)[:, 0, :])
 
@@ -180,7 +180,7 @@ def tile_mix_hidden_by_row_energy_pl_kernel(
 
         def gain_sum(j):
             col = slice(j, j + 1)
-            nc.vector.tensor_scalar(out=denom[:, col], in0=sums[:, col], scalar1=float(R), scalar2=None, op0=ALU.add)
+            nc.scalar.activation(out=denom[:, col], in_=sums[:, col], func=ACT.Copy, bias=float(R))
 
         def gain_recip(j):
             col = slice(j, j + 1)
@@ -252,6 +252,19 @@ def tile_mix_hidden_by_row_energy_pl_kernel(
                 in_=y_ps[j][:].rearrange("p i t -> p t i"),
             )
 
+        def drain_half(j, h):
+            half = slice(h * P // 2, (h + 1) * P // 2)
+            nc.scalar.copy(out=y_out[j][:, :, half], in_=y_ps[j][:, :, half])
+            if h:
+                nc.sync.dma_start(out=out0_view[:, :, tok[j]], in_=y_out[j][:])
+
+        def interleave_half(j, h):
+            half = slice(h * P // 2, (h + 1) * P // 2)
+            nc.vector.tensor_copy(
+                out=y_cols[j][:].rearrange("p (t i) -> p t i", i=PACK)[:, half, :],
+                in_=y_out[j][:].rearrange("p i t -> p t i")[:, half, :],
+            )
+
         def quantise_y(j):
             nc.vector.quantize_mx(
                 out=y_codes[:, tok[j]].bitcast(FP8X4), scales=y_plane[:, tok[j]], in_=y_cols[j][:])
@@ -259,45 +272,45 @@ def tile_mix_hidden_by_row_energy_pl_kernel(
                 pair = slice((j - 1) * P, (j + 1) * P)
                 nc.sync.dma_start(out=out1_view[:, pair], in_=y_codes[:, pair].bitcast(I32))
 
+        deal_wy(0)
+        deal_wy(1)
+        deal_wy(2)
+        deal_wy(3)
         deal_planes()
         z_fp8(0)
-        z_fp8(1)
         z_fp4(0)
         energy(0)
+        gain_sum(0)
+        z_fp8(1)
         z_fp4(1)
         energy(1)
+        gain_sum(1)
         z_fp8(2)
         z_fp4(2)
         energy(2)
+        gain_sum(2)
         z_fp8(3)
         z_fp4(3)
         energy(3)
-        deal_wy(0)
-        gain_sum(0)
-        deal_wy(1)
-        gain_recip(0)
-        deal_wy(2)
-        gain_mult(0)
-        deal_wy(3)
-        gain_sum(1)
-        weigh(0, 0)
-        gain_recip(1)
-        weigh(0, 1)
-        gain_mult(1)
-        gain_sum(2)
-        weigh(1, 0)
-        gain_recip(2)
-        weigh(1, 1)
-        gain_mult(2)
-        deal_wb()
         gain_sum(3)
-        weigh(2, 0)
-        gain_recip(3)
-        weigh(2, 1)
-        gain_mult(3)
+        gain_recip(0)
+        deal_wb()
+        gain_mult(0)
+        gain_recip(1)
+        weigh(0, 0)
+        gain_mult(1)
+        weigh(0, 1)
+        gain_recip(2)
+        weigh(1, 0)
+        gain_mult(2)
+        weigh(1, 1)
         skip(0)
         turn(0)
         gather_words(0)
+        gain_recip(3)
+        weigh(2, 0)
+        gain_mult(3)
+        weigh(2, 1)
         quantise_hid(0)
         weigh(3, 0)
         weigh(3, 1)
@@ -310,24 +323,26 @@ def tile_mix_hidden_by_row_energy_pl_kernel(
         drain(0)
         quantise_hid(1)
         quantise_hid(2)
-        skip(2)
         turn(3)
         gather_words(3)
+        skip(2)
         second(1)
+        second(2)
         drain(1)
         interleave(0)
         quantise_hid(3)
         quantise_y(0)
-        second(2)
         skip(3)
         second(3)
         interleave(1)
         drain(2)
         quantise_y(1)
-        drain(3)
+        drain_half(3, 0)
+        drain_half(3, 1)
         interleave(2)
+        interleave_half(3, 0)
         quantise_y(2)
-        interleave(3)
+        interleave_half(3, 1)
         quantise_y(3)
         for q in range(QUADS):
             queue = nc.scalar if q % 2 else nc.sync

@@ -24,7 +24,6 @@ QUADS = 4
 
 XQ, WC, XT, WA, WY, WB = 0, 1, 2, 4, 6, 8
 PLANES = 9
-WARM_PASSES = 30
 
 
 def tile_mix_hidden_by_row_energy_pl_kernel(
@@ -57,11 +56,15 @@ def tile_mix_hidden_by_row_energy_pl_kernel(
         warm_plane = sbuf("warm_plane", [P, P], U8)
         nc.vector.quantize_mx(out=warm_codes[:].bitcast(FP8X4), scales=warm_plane[:], in_=zeros[:])
         warm_ps = bank("warm_ps", "y2", [P, P])
-        for rep in range(WARM_PASSES):
-            nc.tensor.matmul_mx(
-                out=warm_ps[:], lhsT=warm_codes[:].bitcast(FP8X4), lhsT_scale=warm_plane[:],
-                rhs=warm_codes[:].bitcast(FP8X4), rhs_scale=warm_plane[:], start=True, stop=True,
-            )
+
+        def warm_up(passes, codes):
+            for rep in range(passes):
+                nc.tensor.matmul_mx(
+                    out=warm_ps[:], lhsT=warm_codes[:].bitcast(FP8X4), lhsT_scale=warm_plane[:],
+                    rhs=codes.bitcast(FP8X4), rhs_scale=warm_plane[:], start=True, stop=True,
+                )
+
+        warm_up(12, warm_codes[:])
 
         staged = sbuf("staged", [P, PLANES * W], U8)
         staged_words = staged[4:P:8, :].bitcast(I32).rearrange("q (z c) -> q z c", z=PLANES)
@@ -81,8 +84,6 @@ def tile_mix_hidden_by_row_energy_pl_kernel(
         def fp4_words(words):
             return words.bitcast(I32).rearrange("z p c -> p z c")
 
-        wy_raw = sbuf("wy_raw", [P, 2, 2 * W], U8)
-        nc.scalar.dma_start(out=wy_raw[:].bitcast(I32), in_=fp4_words(wy_words))
         xt = sbuf("xt", [P, 2, W], U32)
         nc.scalar.dma_start(out=xt[:].bitcast(I32), in_=fp8_words(xt_words))
         wa = sbuf("wa", [P, 2, W], U32)
@@ -91,6 +92,8 @@ def tile_mix_hidden_by_row_energy_pl_kernel(
         nc.scalar.dma_start(out=xq[:].bitcast(I32), in_=fp4_words(xq_words)[:, 0, :])
         wc = sbuf("wc", [P, 2 * W], U8)
         nc.scalar.dma_start(out=wc[:].bitcast(I32), in_=fp4_words(wc_words)[:, 0, :])
+        wy_raw = sbuf("wy_raw", [P, 2, 2 * W], U8)
+        nc.scalar.dma_start(out=wy_raw[:].bitcast(I32), in_=fp4_words(wy_words))
 
         for r in range(4):
             nc.sync.dma_start(
@@ -103,9 +106,11 @@ def tile_mix_hidden_by_row_energy_pl_kernel(
         def plane(index, cols):
             return planes[:, index * W + cols.start : index * W + cols.stop]
 
+        warm_up(10, xt[:, 0, 0:P])
         fr_ps = bank("fr_ps", "y3", [P, PACK, P])
         for j in range(PACK):
             nc.tensor.transpose(fr_ps[:, j, :], fr_col[:, j : j + 1].to_broadcast([P, P]), ident[:])
+        warm_up(8, wa[:, 0, 0:P])
         fr_row = sbuf("fr_row", [P, 2, P, 2], F32)
         nc.scalar.activation(
             out=fr_row[:], in_=fr_ps[:].rearrange("m (u e) p -> m u p e", e=2), func=ACT.Copy)
@@ -272,11 +277,10 @@ def tile_mix_hidden_by_row_energy_pl_kernel(
                 pair = slice((j - 1) * P, (j + 1) * P)
                 nc.sync.dma_start(out=out1_view[:, pair], in_=y_codes[:, pair].bitcast(I32))
 
+        deal_planes()
         deal_wy(0)
         deal_wy(1)
         deal_wy(2)
-        deal_wy(3)
-        deal_planes()
         z_fp8(0)
         z_fp4(0)
         energy(0)
@@ -294,7 +298,7 @@ def tile_mix_hidden_by_row_energy_pl_kernel(
         energy(3)
         gain_sum(3)
         gain_recip(0)
-        deal_wb()
+        deal_wy(3)
         gain_mult(0)
         gain_recip(1)
         weigh(0, 0)
@@ -304,45 +308,44 @@ def tile_mix_hidden_by_row_energy_pl_kernel(
         weigh(1, 0)
         gain_mult(2)
         weigh(1, 1)
-        skip(0)
-        turn(0)
-        gather_words(0)
+        deal_wb()
         gain_recip(3)
         weigh(2, 0)
         gain_mult(3)
         weigh(2, 1)
-        quantise_hid(0)
+        skip(0)
+        skip(1)
+        turn(0)
+        turn(1)
+        gather_words(0)
+        gather_words(1)
         weigh(3, 0)
         weigh(3, 1)
-        skip(1)
-        turn(1)
-        turn(2)
-        gather_words(1)
-        gather_words(2)
-        second(0)
-        drain(0)
+        quantise_hid(0)
         quantise_hid(1)
-        quantise_hid(2)
-        turn(3)
-        gather_words(3)
         skip(2)
+        turn(2)
+        turn(3)
+        gather_words(2)
+        gather_words(3)
+        second(0)
         second(1)
-        second(2)
+        drain(0)
         drain(1)
-        interleave(0)
+        quantise_hid(2)
         quantise_hid(3)
-        quantise_y(0)
+        second(2)
         skip(3)
         second(3)
+        interleave(0)
         interleave(1)
+        quantise_y(0)
         drain(2)
-        quantise_y(1)
-        drain_half(3, 0)
-        drain_half(3, 1)
         interleave(2)
-        interleave_half(3, 0)
+        quantise_y(1)
+        drain(3)
         quantise_y(2)
-        interleave_half(3, 1)
+        interleave(3)
         quantise_y(3)
         for q in range(QUADS):
             queue = nc.scalar if q % 2 else nc.sync

from contextlib import ExitStack

import concourse.mybir as mybir
from concourse.masks import make_identity

K, L, T, R, N = 1024, 512, 512, 512, 512
FLOPS = 2 * T * (K * R + L * R + R * N + K * N)

F32 = mybir.dt.float32
BF16 = mybir.dt.bfloat16
I32 = mybir.dt.int32
U32 = mybir.dt.uint32
U8 = mybir.dt.uint8
FP8X4 = mybir.dt.float8_e4m3fn_x4
FP4X4 = mybir.dt.float4_e2m1fn_x4
ALU = mybir.AluOpType
ACT = mybir.ActivationFunctionType

P = 128
PACK = 4
W = 512
TILES = T // P
QUADS = 4

XQ, WC, XT, WA, WY, WB = 0, 1, 2, 4, 6, 8
PLANES = 9


def tile_mix_hidden_by_row_energy_pl_kernel(
    tc, xt_words, xt_scales, wa_words, wa_scales, xq_words, xq_scales, wc_words, wc_scales,
    fr, wb_words, wb_scales, wy_words, wy_scales, out_0, out_1, out_2,
):
    nc = tc.nc

    with ExitStack() as ctx:
        sb = ctx.enter_context(tc.tile_pool(name="sb", bufs=1))
        ps = ctx.enter_context(tc.psum_pool(name="ps", bufs=1))
        ctx.enter_context(tc.manual_schedule())

        def sbuf(name, shape, dtype):
            return sb.tile(shape, dtype, name=name, align_bytes=64)

        def bank(name, tag, shape):
            return ps.tile(shape, F32, name=name, tag=tag)

        fr_col = sbuf("fr_col", [P, PACK], F32)
        nc.gpsimd.dma_start(out=fr_col[:], in_=fr.rearrange("(p j) o -> p (j o)", j=PACK))
        ident = sbuf("ident", [P, P], F32)
        make_identity(nc, ident[:])

        zeros = sbuf("zeros", [P, W], BF16)
        nc.vector.memset(zeros[:], 0.0)
        planes = sbuf("planes", [P, PLANES * W], U8)
        nc.vector.memset(planes[:].bitcast(I32), 0)
        warm_codes = sbuf("warm_codes", [P, P], U32)
        warm_plane = sbuf("warm_plane", [P, P], U8)
        nc.vector.quantize_mx(out=warm_codes[:].bitcast(FP8X4), scales=warm_plane[:], in_=zeros[:])
        warm_ps = bank("warm_ps", "y2", [P, P])

        def warm_up(passes, codes):
            for rep in range(passes):
                nc.tensor.matmul_mx(
                    out=warm_ps[:], lhsT=warm_codes[:].bitcast(FP8X4), lhsT_scale=warm_plane[:],
                    rhs=codes.bitcast(FP8X4), rhs_scale=warm_plane[:], start=True, stop=True,
                )

        warm_up(12, warm_codes[:])

        staged = sbuf("staged", [P, PLANES * W], U8)
        staged_words = staged[4:P:8, :].bitcast(I32).rearrange("q (z c) -> q z c", z=PLANES)
        for first, scales, queue in (
            (XQ, xq_scales, nc.sync), (WC, wc_scales, nc.scalar), (XT, xt_scales, nc.sync),
            (WA, wa_scales, nc.scalar), (WY, wy_scales, nc.sync), (WB, wb_scales, nc.scalar),
        ):
            passes = scales.shape[0]
            queue.dma_start(
                out=staged_words[:, first : first + passes, :],
                in_=scales.bitcast(I32).rearrange("z q c -> q z c"),
            )

        def fp8_words(words):
            return words.rearrange("z p c r -> p z (c r)").bitcast(I32)

        def fp4_words(words):
            return words.bitcast(I32).rearrange("z p c -> p z c")

        xt = sbuf("xt", [P, 2, W], U32)
        nc.scalar.dma_start(out=xt[:].bitcast(I32), in_=fp8_words(xt_words))
        wa = sbuf("wa", [P, 2, W], U32)
        nc.scalar.dma_start(out=wa[:].bitcast(I32), in_=fp8_words(wa_words))
        xq = sbuf("xq", [P, 2 * W], U8)
        nc.scalar.dma_start(out=xq[:].bitcast(I32), in_=fp4_words(xq_words)[:, 0, :])
        wc = sbuf("wc", [P, 2 * W], U8)
        nc.scalar.dma_start(out=wc[:].bitcast(I32), in_=fp4_words(wc_words)[:, 0, :])
        wy_raw = sbuf("wy_raw", [P, 2, 2 * W], U8)
        nc.scalar.dma_start(out=wy_raw[:].bitcast(I32), in_=fp4_words(wy_words))

        for r in range(4):
            nc.sync.dma_start(
                out=planes[r:P:32, :].bitcast(I32),
                in_=staged[8 * r + 4 : P : 32, :].bitcast(I32),
            )
        wb_raw = sbuf("wb_raw", [P, W], U32)
        nc.sync.dma_start(out=wb_raw[:].bitcast(I32), in_=fp8_words(wb_words)[:, 0, :])

        def plane(index, cols):
            return planes[:, index * W + cols.start : index * W + cols.stop]

        warm_up(10, xt[:, 0, 0:P])
        fr_ps = bank("fr_ps", "y3", [P, PACK, P])
        for j in range(PACK):
            nc.tensor.transpose(fr_ps[:, j, :], fr_col[:, j : j + 1].to_broadcast([P, P]), ident[:])
        warm_up(8, wa[:, 0, 0:P])
        fr_row = sbuf("fr_row", [P, 2, P, 2], F32)
        nc.scalar.activation(
            out=fr_row[:], in_=fr_ps[:].rearrange("m (u e) p -> m u p e", e=2), func=ACT.Copy)

        wy = sbuf("wy", [P, 2, 2 * W], U8)
        dealt = sbuf("dealt", [P, 3 * W], U8)
        wb = sbuf("wb", [P, W], U32)

        def deal_wy(part):
            z, half = divmod(part, 2)
            nc.vector.tensor_copy(
                out=wy[:, z, half * W : (half + 1) * W].rearrange("p (i m b) -> p i m b", i=2, b=2),
                in_=wy_raw[:, z, :].rearrange("p (m i b) -> p i m b", i=PACK, b=2)[:, 2 * half : 2 * half + 2, :, :],
            )

        def deal_planes():
            nc.vector.tensor_copy(
                out=dealt[:, 0 : 2 * W].rearrange("p (z i m) -> p z i m", z=2, i=PACK),
                in_=planes[:, WY * W : WB * W].rearrange("p (z m i) -> p z i m", z=2, i=PACK),
            )
            nc.vector.tensor_copy(
                out=dealt[:, 2 * W : 3 * W].rearrange("p (i m) -> p i m", i=PACK),
                in_=planes[:, WB * W : PLANES * W].rearrange("p (m i) -> p i m", i=PACK),
            )

        def deal_wb():
            nc.vector.tensor_copy(
                out=wb[:].bitcast(I32).rearrange("p (i m) -> p i m", i=PACK),
                in_=wb_raw[:].bitcast(I32).rearrange("p (m i) -> p i m", i=PACK),
            )

        all_cols = slice(0, W)
        tok = [slice(j * P, (j + 1) * P) for j in range(TILES)]
        z_ps = [bank("z%d" % j, "z%d" % j, [P, W]) for j in range(TILES)]
        y_ps = {}
        turned = {}
        squares = sbuf("squares", [P, W], BF16)
        sums = sbuf("sums", [P, TILES], F32)
        denom = sbuf("denom", [P, TILES], F32)
        recip = sbuf("recip", [P, TILES], F32)
        gain = sbuf("gain", [P, TILES], F32)
        hid_rows = [sbuf("hid_rows%d" % j, [P, 2, 2 * P], BF16) for j in range(TILES)]
        hid_cols = [sbuf("hid_cols%d" % j, [P, W], BF16) for j in range(TILES)]
        hid_codes = sbuf("hid_codes", [P, W], U32)
        hid_plane = sbuf("hid_plane", [P, W], U8)
        y_out = [sbuf("y_out%d" % j, [P, PACK, P], F32) for j in range(TILES)]
        y_cols = [sbuf("y_cols%d" % j, [P, W], BF16) for j in range(TILES)]
        y_codes = sbuf("y_codes", [P, W], U32)
        y_plane = sbuf("y_plane", [P, W], U8)
        out0_view = out_0.rearrange("(p i) t -> p i t", i=PACK)
        out1_view = out_1[0].rearrange("p c r -> p (c r)").bitcast(I32)

        def z_fp4(j):
            nc.tensor.matmul_mx(
                out=z_ps[j][:],
                lhsT=xq[:, 2 * j * P : 2 * (j + 1) * P].bitcast(FP4X4), lhsT_scale=plane(XQ, tok[j]),
                rhs=wc[:].bitcast(FP4X4), rhs_scale=plane(WC, all_cols),
                start=False, stop=True,
            )

        def z_fp8(j):
            for z in range(2):
                nc.tensor.matmul_mx(
                    out=z_ps[j][:],
                    lhsT=xt[:, z, tok[j]].bitcast(FP8X4), lhsT_scale=plane(XT + z, tok[j]),
                    rhs=wa[:, z, :].bitcast(FP8X4), rhs_scale=plane(WA + z, all_cols),
                    start=(z == 0), stop=False,
                )

        def energy(j):
            nc.scalar.activation(out=squares[:], in_=z_ps[j][:], func=ACT.Square, accum_out=sums[:, j : j + 1])

        def gain_sum(j):
            col = slice(j, j + 1)
            nc.scalar.activation(out=denom[:, col], in_=sums[:, col], func=ACT.Copy, bias=float(R))

        def gain_recip(j):
            col = slice(j, j + 1)
            nc.vector.reciprocal(out=recip[:, col], in_=denom[:, col])

        def gain_mult(j):
            col = slice(j, j + 1)
            nc.vector.tensor_tensor(out=gain[:, col], in0=sums[:, col], in1=recip[:, col], op=ALU.mult)

        def weigh(j, u):
            nc.vector.scalar_tensor_tensor(
                out=hid_rows[j][:, u, :].rearrange("t (p e) -> t p e", e=2),
                in0=z_ps[j][:].rearrange("t (p i) -> t p i", i=PACK)[:, :, 2 * u : 2 * u + 2],
                scalar=gain[:, j : j + 1],
                in1=fr_row[:, u, :, :],
                op0=ALU.mult, op1=ALU.mult,
            )

        def turn(j):
            turned[j] = bank("turned%d" % j, "z%d" % j, [P, 2, P])
            for u in range(2):
                nc.tensor.transpose(turned[j][:, u, :], hid_rows[j][:, u, :].bitcast(F32), ident[:])

        def gather_words(j):
            nc.scalar.copy(
                out=hid_cols[j][:].bitcast(F32).rearrange("p (t u) -> p t u", u=2),
                in_=turned[j][:].rearrange("p u t -> p t u"),
            )

        def quantise_hid(j):
            nc.vector.quantize_mx(
                out=hid_codes[:, tok[j]].bitcast(FP8X4), scales=hid_plane[:, tok[j]], in_=hid_cols[j][:])

        def skip(j):
            y_ps[j] = bank("y%d" % j, "y%d" % j, [P, PACK, P])
            for z in range(2):
                for i in range(PACK):
                    nc.tensor.matmul_mx(
                        out=y_ps[j][:, i, :],
                        lhsT=wy[:, z, 2 * i * P : 2 * (i + 1) * P].bitcast(FP4X4),
                        lhsT_scale=dealt[:, z * W + i * P : z * W + (i + 1) * P],
                        rhs=xt[:, z, tok[j]].bitcast(FP8X4), rhs_scale=plane(XT + z, tok[j]),
                        start=(z == 0 and i == 0), stop=False,
                    )

        def second(j):
            for i in range(PACK):
                nc.tensor.matmul_mx(
                    out=y_ps[j][:, i, :],
                    lhsT=wb[:, i * P : (i + 1) * P].bitcast(FP8X4),
                    lhsT_scale=dealt[:, 2 * W + i * P : 2 * W + (i + 1) * P],
                    rhs=hid_codes[:, tok[j]].bitcast(FP8X4), rhs_scale=hid_plane[:, tok[j]],
                    start=False, stop=(i == PACK - 1),
                )

        def drain(j):
            nc.scalar.copy(out=y_out[j][:], in_=y_ps[j][:])
            nc.sync.dma_start(out=out0_view[:, :, tok[j]], in_=y_out[j][:])

        def interleave(j):
            nc.vector.tensor_copy(
                out=y_cols[j][:].rearrange("p (t i) -> p t i", i=PACK),
                in_=y_out[j][:].rearrange("p i t -> p t i"),
            )

        def interleave_from_psum(j):
            nc.vector.tensor_copy(
                out=y_cols[j][:].rearrange("p (t i) -> p t i", i=PACK),
                in_=y_ps[j][:].rearrange("p i t -> p t i"),
            )

        def drain_half(j, h):
            half = slice(h * P // 2, (h + 1) * P // 2)
            nc.scalar.copy(out=y_out[j][:, :, half], in_=y_ps[j][:, :, half])
            if h:
                nc.sync.dma_start(out=out0_view[:, :, tok[j]], in_=y_out[j][:])

        def interleave_half(j, h):
            half = slice(h * P // 2, (h + 1) * P // 2)
            nc.vector.tensor_copy(
                out=y_cols[j][:].rearrange("p (t i) -> p t i", i=PACK)[:, half, :],
                in_=y_out[j][:].rearrange("p i t -> p t i")[:, half, :],
            )

        def quantise_y(j):
            nc.vector.quantize_mx(
                out=y_codes[:, tok[j]].bitcast(FP8X4), scales=y_plane[:, tok[j]], in_=y_cols[j][:])
            if j % 2:
                pair = slice((j - 1) * P, (j + 1) * P)
                nc.sync.dma_start(out=out1_view[:, pair], in_=y_codes[:, pair].bitcast(I32))

        deal_planes()
        deal_wy(0)
        deal_wy(1)
        deal_wy(2)
        z_fp8(0)
        z_fp4(0)
        energy(0)
        gain_sum(0)
        z_fp8(1)
        z_fp4(1)
        energy(1)
        gain_sum(1)
        z_fp8(2)
        z_fp4(2)
        energy(2)
        gain_sum(2)
        z_fp8(3)
        z_fp4(3)
        energy(3)
        gain_sum(3)
        gain_recip(0)
        deal_wy(3)
        gain_mult(0)
        gain_recip(1)
        weigh(0, 0)
        gain_mult(1)
        weigh(0, 1)
        gain_recip(2)
        weigh(1, 0)
        gain_mult(2)
        weigh(1, 1)
        deal_wb()
        gain_recip(3)
        weigh(2, 0)
        gain_mult(3)
        weigh(2, 1)
        skip(0)
        skip(1)
        turn(0)
        turn(1)
        gather_words(0)
        gather_words(1)
        weigh(3, 0)
        weigh(3, 1)
        quantise_hid(0)
        quantise_hid(1)
        skip(2)
        turn(2)
        turn(3)
        gather_words(2)
        gather_words(3)
        second(0)
        second(1)
        drain(0)
        drain(1)
        quantise_hid(2)
        quantise_hid(3)
        second(2)
        skip(3)
        second(3)
        interleave(0)
        interleave(1)
        quantise_y(0)
        drain(2)
        interleave(2)
        quantise_y(1)
        drain(3)
        quantise_y(2)
        interleave(3)
        quantise_y(3)
        for q in range(QUADS):
            queue = nc.scalar if q % 2 else nc.sync
            queue.dma_start(
                out=out_2[0, 4 * q : 4 * q + 4, :].bitcast(I32),
                in_=y_plane[32 * q : 32 * q + 4, :].bitcast(I32),
            )
